import numpy as np
import ml_dtypes


def mxq(x, axis, fmt="e4m3"):
    dtype, down = {"e4m3": (ml_dtypes.float8_e4m3fn, 7), "e5m2": (ml_dtypes.float8_e5m2, 14)}[fmt]
    v = np.moveaxis(np.asarray(x, np.float32).astype(ml_dtypes.bfloat16).astype(np.float64), axis, -1)
    blocks = v.reshape(v.shape[:-1] + (-1, 32))
    amax = np.abs(blocks).max(-1, keepdims=True)
    byte = np.maximum(np.where(amax > 0, np.frexp(amax)[1] - 1 + 127, 0) - down, 1)
    scale = np.exp2(byte - 127.0)
    codes = (blocks / scale).astype(np.float32).astype(dtype).astype(np.float64)
    return np.moveaxis((codes * scale).reshape(v.shape), -1, axis)


WIDE = False


def mx_kscale(k):
    if not WIDE:
        return np.ones(k)
    levels = np.array([10, -10, 5, -5, 0])
    if k % 512:
        return np.exp2(np.random.permutation(np.resize(levels, k // 32))).repeat(32)
    a = np.empty((k // 512, 16))
    for p in range(k // 512):
        a[p, :8] = np.random.permutation(np.resize(levels, 8))
        for g in range(8):
            far = levels[np.abs(levels - a[p, g]) >= 10]
            a[p, g + 8] = far[np.random.randint(len(far))]
    return np.exp2(a.ravel()).repeat(32)


def f64(x):
    return np.asarray(x).astype(np.float64)


def striped(idx):
    return np.tile(idx.reshape(-1, 16).T, (8, 1)).astype(np.uint16)


def unstriped(offs):
    return offs[:16].T.reshape(-1).astype(np.int64)


E2M1 = np.array([0.0, 0.5, 1.0, 1.5, 2.0, 3.0, 4.0, 6.0, -0.0, -0.5, -1.0, -1.5, -2.0, -3.0, -4.0, -6.0])


def pack_weight(w, fmt):
    k, n = w.shape
    w = f64(np.asarray(w, np.float32).astype(ml_dtypes.bfloat16)).reshape(k // 32, 32, n)
    amax = np.abs(w).max(1)
    if fmt == "e4m3":
        byte = np.frexp(amax)[1] - 1 + 127 - 7
    else:
        mant, ex = np.frexp(amax / 6.0)
        byte = np.where(mant > 0.5, ex, ex - 1) + 127
    byte = np.clip(np.where(amax > 0, byte, 1), 1, 254)
    scaled = (w * np.exp2(127.0 - byte)[:, None, :]).reshape(k, n).astype(np.float32)
    by_word = np.ascontiguousarray(scaled.reshape(k // 512, 128, 4, n).transpose(0, 1, 3, 2))
    if fmt == "e4m3":
        words = by_word.astype(ml_dtypes.float8_e4m3fn).view(np.uint8)
    else:
        c = by_word.astype(ml_dtypes.float4_e2m1fn).view(np.uint8) & 0xF
        words = (c[..., 0::2] | (c[..., 1::2] << 4)).reshape(k // 512, 128, 2 * n)
    return np.ascontiguousarray(words), np.ascontiguousarray(byte.astype(np.uint8).reshape(k // 512, 16, n))


def unpack_weight(words, scales, fmt):
    g, _, n = scales.shape
    words = np.ascontiguousarray(words).reshape(g, 128, n, -1)
    if fmt == "e4m3":
        vals = words.view(ml_dtypes.float8_e4m3fn).astype(np.float64)
    else:
        nib = np.empty((g, 128, n, 4), np.uint8)
        nib[..., 0::2] = words & 0xF
        nib[..., 1::2] = words >> 4
        vals = E2M1[nib]
    vals = vals * np.repeat(np.exp2(scales.astype(np.float64) - 127.0), 8, axis=1)[..., None]
    return vals.transpose(0, 1, 3, 2).reshape(g * 512, n)


def gelu(v):
    return 0.5 * v * (1.0 + np.tanh(np.sqrt(2.0 / np.pi) * (v + 0.044715 * v**3)))


K, K2, T, T2, S, P, H, N = 1024, 512, 4096, 2048, 1024, 512, 1024, 512


def setup_inputs():
    n = np.random.standard_normal
    s = mx_kscale(K)[:, None]
    s2 = mx_kscale(K2)[:, None]
    u = mx_kscale(H)[:, None]
    d = {}
    d["tab_words"], d["tab_scales"] = pack_weight(n((K, T)) * s, "e4m3")
    d["offs"] = striped(np.random.permutation(T)[:S])
    d["tab2_words"], d["tab2_scales"] = pack_weight(n((K2, T2)) * s2, "e4m3")
    d["offs2"] = striped(np.random.permutation(T2)[:P])
    d["pos1"] = striped(np.random.permutation(S)[:P])
    d["wa"] = (1.8 * n((K, H)) / K**0.5 / s).astype(np.float32)
    d["ga"] = np.exp(0.4 * n(H)).astype(np.float32)
    d["wb_words"], d["wb_scales"] = pack_weight(1.6 * n((K2, H)) / K2**0.5 / s2, "e2m1")
    d["wgs"] = np.exp(0.3 * n((128, P))).astype(np.float32)
    d["cap"] = (0.7 + 0.7 * n((H, S))).astype(np.float32)
    d["gz"] = (np.exp(0.4 * n(H)) * u[:, 0]).astype(np.float32)
    d["wc"] = (n((H, N)) / H**0.5 / u).astype(np.float32)
    return d


def reference(tab_words, tab_scales, offs, tab2_words, tab2_scales, offs2, pos1, wa, ga, wb_words, wb_scales, wgs, cap, gz, wc):
    v = unpack_weight(tab_words, tab_scales, "e4m3")[:, unstriped(offs)]
    v2 = unpack_weight(tab2_words, tab2_scales, "e4m3")[:, unstriped(offs2)]
    y = mxq(f64(wa), 0, "e4m3").T @ v
    a = f64(ga)[:, None] * (y / (1.0 + np.exp(-y)))
    y2 = unpack_weight(wb_words, wb_scales, "e2m1").T @ v2
    b = np.log(1.0 + np.square(y2))
    placed = np.zeros((H, S))
    placed[:, unstriped(pos1)] = np.tile(f64(wgs), (H // 128, 1)) * b
    z = f64(gz)[:, None] * (np.minimum(a, f64(cap)) + placed)
    return mxq(f64(wc), 0, "e4m3").T @ mxq(z, 0, "e4m3")

@@ -1,0 +1,284 @@
+from contextlib import ExitStack
+
+import concourse.mybir as mybir
+
+K, K2, T, T2, S, NP, H, N = 1024, 512, 4096, 2048, 1024, 512, 1024, 512
+FLOPS = 2 * (K * H * S + K2 * H * NP + H * N * S)
+
+F32 = mybir.dt.float32
+BF16 = mybir.dt.bfloat16
+I32 = mybir.dt.int32
+U32 = mybir.dt.uint32
+U16 = mybir.dt.uint16
+U8 = mybir.dt.uint8
+FP8X4 = mybir.dt.float8_e4m3fn_x4
+FP4X4 = mybir.dt.float4_e2m1fn_x4
+ALU = mybir.AluOpType
+ACT = mybir.ActivationFunctionType
+
+P = 128
+PACK = 4
+BANK = 512
+LAST_CHUNKS = ((0, 512), (512, 256), (768, 256))
+
+
+def tile_list_airway_hazard_features_kernel(
+    tc, tab_words, tab_scales, offs, tab2_words, tab2_scales, offs2, pos1,
+    wa, ga, wb_words, wb_scales, wgs, cap, gz, wc, out,
+):
+    nc = tc.nc
+    with ExitStack() as ctx:
+        lists = ctx.enter_context(tc.tile_pool(name="lists", bufs=1))
+        keep = ctx.enter_context(tc.tile_pool(name="keep", bufs=1))
+        psum = ctx.enter_context(tc.psum_pool(name="psum", bufs=4))
+
+        def tile(shape, dtype, name, tag=None, bufs=1):
+            return keep.tile(shape, dtype, name=name, tag=tag or name, bufs=bufs, align_bytes=64)
+
+        def load_planes(plane, scales):
+            rows = PACK * scales.shape[0]
+            for q in range(4):
+                nc.sync.dma_start(
+                    plane[32 * q : 32 * q + rows, :].bitcast(I32),
+                    scales[:, 4 * q : 4 * q + 4, :].bitcast(I32),
+                )
+
+        def words_of(words, a):
+            return words[a].rearrange("p n t -> p (n t)").bitcast(I32)
+
+        tab2_sc = tile([P, T2], U8, "tab2_sc")
+        wb_sc_raw = tile([P, H], U8, "wb_sc_raw")
+        tab_sc = tile([P, T], U8, "tab_sc")
+        nc.vector.memset(tab2_sc[:].bitcast(I32), 0)
+        nc.vector.memset(wb_sc_raw[:].bitcast(I32), 0)
+        warm = tile([P, 8], F32, "warm")
+        nc.gpsimd.memset(warm[:, 0:1], 1.0)
+        nc.scalar.activation(warm[:, 1:2], warm[:, 0:1], ACT.Ln)
+
+        tab2_w = tile([P, T2], U32, "tab2_w", tag="eight")
+        nc.sync.dma_start(tab2_w[:].bitcast(I32), words_of(tab2_words, 0))
+        offs2_t = lists.tile([P, NP // 16], U16, name="offs2_t")
+        nc.sync.dma_start(offs2_t[:], offs2)
+        wb_raw = tile([P, 2 * H], U8, "wb_raw")
+        nc.sync.dma_start(wb_raw[:].bitcast(I32), wb_words[0].bitcast(I32))
+        load_planes(tab2_sc, tab2_scales)
+        load_planes(wb_sc_raw, wb_scales)
+        gz_t = tile([P, 2, PACK], F32, "gz_t")
+        ga_t = tile([P, 2, PACK], F32, "ga_t")
+        nc.gpsimd.dma_start(gz_t[:], gz.rearrange("(b p t) -> p b t", b=2, t=PACK))
+        nc.gpsimd.dma_start(ga_t[:], ga.rearrange("(b p t) -> p b t", b=2, t=PACK))
+        wgs_t = tile([P, PACK, NP], F32, "wgs_t")
+        for q in (0, 2, 1, 3):
+            nc.sync.dma_start(wgs_t[32 * q : 32 * q + 32], wgs.rearrange("(u t) j -> u t j", t=PACK))
+        pos1_t = lists.tile([P, NP // 16], U16, name="pos1_t")
+        nc.sync.dma_start(pos1_t[:], pos1)
+        offs_t = lists.tile([P, S // 16], U16, name="offs_t")
+        nc.sync.dma_start(offs_t[:], offs)
+        nc.vector.memset(tab_sc[:].bitcast(I32), 0)
+
+        tab_w = []
+        for a in range(2):
+            w = tile([P, T], U32, "tab_w%d" % a, tag="big%d" % a)
+            nc.sync.dma_start(w[:].bitcast(I32), words_of(tab_words, a))
+            tab_w.append(w)
+            if a == 0:
+                load_planes(tab_sc, tab_scales)
+
+        wa_raw = {}
+        cap_t = {}
+
+        def load_wa(a, b):
+            wa_raw[a, b] = tile([P, PACK, BANK], F32, "wa_raw%d%d" % (a, b), tag="wa%d%d" % (a, b))
+            nc.sync.dma_start(
+                wa_raw[a, b][:],
+                wa[512 * a : 512 * (a + 1), 512 * b : 512 * (b + 1)].rearrange("(p i) c -> p i c", i=PACK),
+            )
+
+        def load_cap(b, tag):
+            cap_t[b] = tile([P, PACK, S], F32, "cap%d" % b, tag=tag)
+            rows = cap[512 * b : 512 * (b + 1), :].rearrange("(p t) j -> p t j", t=PACK)
+            for h in range(2):
+                nc.sync.dma_start(cap_t[b][:, 2 * h : 2 * h + 2, :], rows[:, 2 * h : 2 * h + 2, :])
+
+        wb_codes = tile([P, 2 * H], U8, "wb_codes")
+        wb_sc = tile([P, H], U8, "wb_sc")
+        nc.vector.tensor_copy(
+            wb_codes[:].rearrange("p (b t m e) -> p b t m e", b=2, t=PACK, e=2),
+            wb_raw[:].rearrange("p (b m t e) -> p b t m e", b=2, t=PACK, e=2),
+        )
+        nc.vector.tensor_copy(
+            wb_sc[:].rearrange("p (b t m) -> p b t m", b=2, t=PACK),
+            wb_sc_raw[:].rearrange("p (b m t) -> p b t m", b=2, t=PACK),
+        )
+        v2 = tile([P, NP], U32, "v2")
+        v2_sc = tile([P, NP], U8, "v2_sc")
+        nc.vector.tensor_copy(v2[:], tab2_w[:].indirect(offs2_t[:]))
+        nc.vector.tensor_copy(v2_sc[:], tab2_sc[:].indirect(offs2_t[:]))
+
+        pages = []
+        for t in range(PACK):
+            page = tile([P, S], F32, "page%d" % t)
+            nc.vector.memset(page[:], 0.0)
+            pages.append(page)
+
+        gas = {}
+        for b in range(2):
+            for t in range(PACK):
+                s = PACK * b + t
+                acc = psum.tile([P, NP], F32, name="acc", tag="acc")
+                nc.tensor.matmul_mx(
+                    out=acc[:],
+                    lhsT=wb_codes[:, 2 * P * s : 2 * P * (s + 1)].bitcast(FP4X4),
+                    lhsT_scale=wb_sc[:, P * s : P * (s + 1)],
+                    rhs=v2[:].bitcast(FP8X4),
+                    rhs_scale=v2_sc[:],
+                    start=True,
+                    stop=True,
+                )
+                gas[b, t] = tile([P, NP], F32, "gas%d%d" % (b, t))
+                nc.scalar.activation(gas[b, t][:], acc[:], ACT.Square)
+                nc.scalar.activation(gas[b, t][:], gas[b, t][:], ACT.Ln, bias=1.0)
+
+        def scatter(b, t, weight):
+            nc.vector.tensor_tensor(pages[t][:].indirect(pos1_t[:]), gas[b, t][:], weight, ALU.mult)
+
+        for t in range(PACK - 1):
+            weight = tile([P, NP], F32, "weight%d" % t)
+            nc.vector.tensor_scalar(weight[:], wgs_t[:, t, :], gz_t[:, 0, t : t + 1], None, ALU.mult)
+            scatter(0, t, weight[:])
+
+        v = [tile([P, S], U32, "v%d" % a) for a in range(2)]
+        v_sc = tile([P, S], U8, "v_sc")
+        nc.vector.tensor_copy(v[0][:], tab_w[0][:].indirect(offs_t[:]))
+        nc.vector.tensor_copy(v_sc[:], tab_sc[:].indirect(offs_t[:]))
+        nc.vector.tensor_copy(v[1][:], tab_w[1][:].indirect(offs_t[:]))
+
+        load_wa(0, 0)
+        load_wa(1, 0)
+        load_cap(0, "cap0")
+        load_wa(0, 1)
+        load_wa(1, 1)
+        wc_raw = tile([P, 2, PACK, N], F32, "wc_raw", tag="big0")
+        for b in range(2):
+            nc.sync.dma_start(wc_raw[:, b], wc[512 * b : 512 * (b + 1), :].rearrange("(p t) n -> p t n", t=PACK))
+        load_cap(1, "big1")
+
+        def quantize(name, staged, width):
+            codes = tile([P, width], U32, name + "_codes")
+            plane = tile([P, width], U8, name + "_sc")
+            nc.vector.quantize_mx(out=codes[:].bitcast(FP8X4), scales=plane[:], in_=staged)
+            return codes, plane
+
+        wa_q = {}
+
+        def quantize_wa(a, b, staged):
+            nc.scalar.copy(
+                staged.rearrange("p (t m i) -> p m i t", t=PACK, i=PACK),
+                wa_raw[a, b][:].rearrange("p i (m t) -> p m i t", t=PACK),
+            )
+            wa_q[a, b] = quantize("wa%d%d" % (a, b), staged, BANK)
+
+        def staging():
+            return tile([P, PACK * BANK], BF16, "staged", bufs=2)
+
+        quantize_wa(0, 0, staging()[:])
+        held = tile([P, 2 * BANK], F32, "held")
+        quantize_wa(1, 0, held[:].bitcast(BF16))
+        t = PACK - 1
+        nc.vector.tensor_scalar(held[:, 0:NP], wgs_t[:, t, :], gz_t[:, 0, t : t + 1], None, ALU.mult)
+        scatter(0, t, held[:, 0:NP])
+
+        def sensor_features(b, t):
+            act = tile([P, S], F32, "act", bufs=5)
+            for h in range(2):
+                cols = slice(BANK * h, BANK * (h + 1))
+                acc = psum.tile([P, BANK], F32, name="acc", tag="acc")
+                for a in range(2):
+                    codes, plane = wa_q[a, b]
+                    nc.tensor.matmul_mx(
+                        out=acc[:],
+                        lhsT=codes[:, P * t : P * (t + 1)].bitcast(FP8X4),
+                        lhsT_scale=plane[:, P * t : P * (t + 1)],
+                        rhs=v[a][:, cols].bitcast(FP8X4),
+                        rhs_scale=v_sc[4 * a : P, cols],
+                        start=(a == 0),
+                        stop=(a == 1),
+                    )
+                nc.scalar.activation(act[:, cols], acc[:], ACT.Silu)
+            return act
+
+        def cap_and_add(b, acts, z_rows, cols):
+            def capped(t):
+                nc.vector.scalar_tensor_tensor(
+                    acts[t][:, cols], acts[t][:, cols], ga_t[:, b, t : t + 1], cap_t[b][:, t, cols], ALU.mult, ALU.min
+                )
+
+            capped(0)
+            for t in range(PACK):
+                if t + 1 < PACK:
+                    capped(t + 1)
+                nc.vector.scalar_tensor_tensor(
+                    z_rows[:, t, cols], acts[t][:, cols], gz_t[:, b, t : t + 1], pages[t][:, cols], ALU.mult, ALU.add
+                )
+
+        def interleave(copy, staged, rows):
+            copy(
+                staged.rearrange("p (c e t) -> p c t e", e=4, t=PACK),
+                rows.rearrange("p t (c e) -> p c t e", e=4),
+            )
+
+        acts = [sensor_features(0, t) for t in range(PACK)]
+        quantize_wa(0, 1, staging()[:])
+        quantize_wa(1, 1, staging()[:])
+        z_rows = tile([P, PACK, S], BF16, "z_rows0", tag="eight")
+        cap_and_add(0, acts, z_rows, slice(0, S))
+
+        for t in range(PACK):
+            nc.scalar.activation(wgs_t[:, t, :], wgs_t[:, t, :], ACT.Copy, scale=gz_t[:, 1, t : t + 1])
+        acts = [sensor_features(1, t) for t in range(PACK)]
+        z0_codes = tile([P, S], U32, "z0_codes")
+        z0_sc = tile([P, S], U8, "z0_sc")
+        for h in range(2):
+            cols = slice(BANK * h, BANK * (h + 1))
+            staged = staging()
+            interleave(nc.scalar.copy, staged[:], z_rows[:, :, cols])
+            nc.vector.quantize_mx(out=z0_codes[:, cols].bitcast(FP8X4), scales=z0_sc[:, cols], in_=staged[:])
+        wc_q = []
+        for b in range(2):
+            staged = staging()
+            interleave(nc.scalar.copy, staged[:], wc_raw[:, b])
+            wc_q.append(quantize("wc%d" % b, staged[:], N))
+        for t in range(PACK):
+            scatter(1, t, wgs_t[:, t, :])
+
+        z_rows = tile([P, PACK, S], BF16, "z_rows1", tag="eight")
+        out_rows = out.rearrange("(c p) j -> p c j", p=P)
+        for i, (j0, width) in enumerate(LAST_CHUNKS):
+            cols = slice(j0, j0 + width)
+            last = i == len(LAST_CHUNKS) - 1
+            banks = [psum.tile([P, BANK], F32, name="res", tag=("res", "acc")[i % 2]) for c in range(4)]
+
+            def product(b, codes, plane):
+                for c in range(4):
+                    nc.tensor.matmul_mx(
+                        out=banks[c][:, 0:width],
+                        lhsT=wc_q[b][0][:, P * c : P * (c + 1)].bitcast(FP8X4),
+                        lhsT_scale=wc_q[b][1][:, P * c : P * (c + 1)],
+                        rhs=codes.bitcast(FP8X4),
+                        rhs_scale=plane,
+                        start=(b == 0),
+                        stop=(b == 1),
+                    )
+
+            product(0, z0_codes[:, cols], z0_sc[:, cols])
+            cap_and_add(1, acts, z_rows, cols)
+            staged = staging()
+            interleave(nc.vector.tensor_copy if last else nc.scalar.copy, staged[:, 0 : PACK * width], z_rows[:, :, cols])
+            codes, plane = quantize("z1%d" % i, staged[:, 0 : PACK * width], width)
+            product(1, codes[:], plane[:])
+            for half in range(2):
+                result = tile([P, 2, width], F32, "result%d%d" % (i, half), tag=(("wa00", "wa10"), ("wa01", "wa11"), ("big0", "cap0"))[i][half])
+                for c in range(2):
+                    copy = nc.vector.tensor_copy if last and half == 1 else nc.scalar.copy
+                    copy(result[:, c, :], banks[2 * half + c][:, 0:width])
+                nc.sync.dma_start(out_rows[:, 2 * half : 2 * half + 2, cols], result[:])

@@ -19,7 +19,7 @@ ACT = mybir.ActivationFunctionType
 P = 128
 PACK = 4
 BANK = 512
-LAST_CHUNKS = ((0, 512), (512, 256), (768, 256))
+LAST_CHUNKS = ((0, 256), (256, 256), (512, 256), (768, 128), (896, 128))
 
 
 def tile_list_airway_hazard_features_kernel(
@@ -35,10 +35,10 @@ def tile_list_airway_hazard_features_kernel(
         def tile(shape, dtype, name, tag=None, bufs=1):
             return keep.tile(shape, dtype, name=name, tag=tag or name, bufs=bufs, align_bytes=64)
 
-        def load_planes(plane, scales):
+        def load_planes(queue, plane, scales):
             rows = PACK * scales.shape[0]
             for q in range(4):
-                nc.sync.dma_start(
+                queue.dma_start(
                     plane[32 * q : 32 * q + rows, :].bitcast(I32),
                     scales[:, 4 * q : 4 * q + 4, :].bitcast(I32),
                 )
@@ -49,40 +49,39 @@ def tile_list_airway_hazard_features_kernel(
         tab2_sc = tile([P, T2], U8, "tab2_sc")
         wb_sc_raw = tile([P, H], U8, "wb_sc_raw")
         tab_sc = tile([P, T], U8, "tab_sc")
-        nc.vector.memset(tab2_sc[:].bitcast(I32), 0)
-        nc.vector.memset(wb_sc_raw[:].bitcast(I32), 0)
+        nc.gpsimd.memset(tab2_sc[:].bitcast(I32), 0)
+        nc.gpsimd.memset(wb_sc_raw[:].bitcast(I32), 0)
+        nc.gpsimd.memset(tab_sc[:].bitcast(I32), 0)
         warm = tile([P, 8], F32, "warm")
-        nc.gpsimd.memset(warm[:, 0:1], 1.0)
+        nc.vector.memset(warm[:, 0:1], 1.0)
         nc.scalar.activation(warm[:, 1:2], warm[:, 0:1], ACT.Ln)
 
         tab2_w = tile([P, T2], U32, "tab2_w", tag="eight")
         nc.sync.dma_start(tab2_w[:].bitcast(I32), words_of(tab2_words, 0))
-        offs2_t = lists.tile([P, NP // 16], U16, name="offs2_t")
-        nc.sync.dma_start(offs2_t[:], offs2)
         wb_raw = tile([P, 2 * H], U8, "wb_raw")
         nc.sync.dma_start(wb_raw[:].bitcast(I32), wb_words[0].bitcast(I32))
-        load_planes(tab2_sc, tab2_scales)
-        load_planes(wb_sc_raw, wb_scales)
+        offs2_t = lists.tile([P, NP // 16], U16, name="offs2_t")
+        nc.sync.dma_start(offs2_t[:], offs2)
+        load_planes(nc.sync, tab2_sc, tab2_scales)
+        load_planes(nc.sync, wb_sc_raw, wb_scales)
         gz_t = tile([P, 2, PACK], F32, "gz_t")
         ga_t = tile([P, 2, PACK], F32, "ga_t")
-        nc.gpsimd.dma_start(gz_t[:], gz.rearrange("(b p t) -> p b t", b=2, t=PACK))
-        nc.gpsimd.dma_start(ga_t[:], ga.rearrange("(b p t) -> p b t", b=2, t=PACK))
-        wgs_t = tile([P, PACK, NP], F32, "wgs_t")
-        for q in (0, 2, 1, 3):
-            nc.sync.dma_start(wgs_t[32 * q : 32 * q + 32], wgs.rearrange("(u t) j -> u t j", t=PACK))
+        nc.sync.dma_start(gz_t[:], gz.rearrange("(b p t) -> p b t", b=2, t=PACK))
         pos1_t = lists.tile([P, NP // 16], U16, name="pos1_t")
         nc.sync.dma_start(pos1_t[:], pos1)
         offs_t = lists.tile([P, S // 16], U16, name="offs_t")
         nc.sync.dma_start(offs_t[:], offs)
-        nc.vector.memset(tab_sc[:].bitcast(I32), 0)
+        nc.sync.dma_start(ga_t[:], ga.rearrange("(b p t) -> p b t", b=2, t=PACK))
+        wgs_t = tile([P, PACK, NP], F32, "wgs_t")
+        for q in (0, 2, 1, 3):
+            nc.sync.dma_start(wgs_t[32 * q : 32 * q + 32], wgs.rearrange("(u t) j -> u t j", t=PACK))
+        load_planes(nc.sync, tab_sc, tab_scales)
 
         tab_w = []
         for a in range(2):
             w = tile([P, T], U32, "tab_w%d" % a, tag="big%d" % a)
             nc.sync.dma_start(w[:].bitcast(I32), words_of(tab_words, a))
             tab_w.append(w)
-            if a == 0:
-                load_planes(tab_sc, tab_scales)
 
         wa_raw = {}
         cap_t = {}
@@ -103,17 +102,17 @@ def tile_list_airway_hazard_features_kernel(
         wb_codes = tile([P, 2 * H], U8, "wb_codes")
         wb_sc = tile([P, H], U8, "wb_sc")
         nc.vector.tensor_copy(
-            wb_codes[:].rearrange("p (b t m e) -> p b t m e", b=2, t=PACK, e=2),
-            wb_raw[:].rearrange("p (b m t e) -> p b t m e", b=2, t=PACK, e=2),
-        )
-        nc.vector.tensor_copy(
-            wb_sc[:].rearrange("p (b t m) -> p b t m", b=2, t=PACK),
-            wb_sc_raw[:].rearrange("p (b m t) -> p b t m", b=2, t=PACK),
+            wb_codes[:].bitcast(U16).rearrange("p (b t m) -> p b t m", b=2, t=PACK),
+            wb_raw[:].bitcast(U16).rearrange("p (b m t) -> p b t m", b=2, t=PACK),
         )
         v2 = tile([P, NP], U32, "v2")
         v2_sc = tile([P, NP], U8, "v2_sc")
         nc.vector.tensor_copy(v2[:], tab2_w[:].indirect(offs2_t[:]))
         nc.vector.tensor_copy(v2_sc[:], tab2_sc[:].indirect(offs2_t[:]))
+        nc.vector.tensor_copy(
+            wb_sc[:].rearrange("p (b t m) -> p b t m", b=2, t=PACK),
+            wb_sc_raw[:].rearrange("p (b m t) -> p b t m", b=2, t=PACK),
+        )
 
         pages = []
         for t in range(PACK):
@@ -149,8 +148,8 @@ def tile_list_airway_hazard_features_kernel(
 
         v = [tile([P, S], U32, "v%d" % a) for a in range(2)]
         v_sc = tile([P, S], U8, "v_sc")
-        nc.vector.tensor_copy(v[0][:], tab_w[0][:].indirect(offs_t[:]))
         nc.vector.tensor_copy(v_sc[:], tab_sc[:].indirect(offs_t[:]))
+        nc.vector.tensor_copy(v[0][:], tab_w[0][:].indirect(offs_t[:]))
         nc.vector.tensor_copy(v[1][:], tab_w[1][:].indirect(offs_t[:]))
 
         load_wa(0, 0)
@@ -245,17 +244,19 @@ def tile_list_airway_hazard_features_kernel(
             nc.vector.quantize_mx(out=z0_codes[:, cols].bitcast(FP8X4), scales=z0_sc[:, cols], in_=staged[:])
         wc_q = []
         for b in range(2):
-            staged = staging()
+            staged = tile([P, PACK * N], BF16, "wc_staged%d" % b, tag="wa%d0" % b)
             interleave(nc.scalar.copy, staged[:], wc_raw[:, b])
             wc_q.append(quantize("wc%d" % b, staged[:], N))
         for t in range(PACK):
             scatter(1, t, wgs_t[:, t, :])
 
         z_rows = tile([P, PACK, S], BF16, "z_rows1", tag="eight")
+        spent = ("wa01", "wa11", "wa00", "wa10", "big0", "cap0")
         out_rows = out.rearrange("(c p) j -> p c j", p=P)
         for i, (j0, width) in enumerate(LAST_CHUNKS):
             cols = slice(j0, j0 + width)
             last = i == len(LAST_CHUNKS) - 1
+            narrow = width < 256
             banks = [psum.tile([P, BANK], F32, name="res", tag=("res", "acc")[i % 2]) for c in range(4)]
 
             def product(b, codes, plane):
@@ -273,12 +274,13 @@ def tile_list_airway_hazard_features_kernel(
             product(0, z0_codes[:, cols], z0_sc[:, cols])
             cap_and_add(1, acts, z_rows, cols)
             staged = staging()
-            interleave(nc.vector.tensor_copy if last else nc.scalar.copy, staged[:, 0 : PACK * width], z_rows[:, :, cols])
+            interleave(nc.vector.tensor_copy if narrow else nc.scalar.copy, staged[:, 0 : PACK * width], z_rows[:, :, cols])
             codes, plane = quantize("z1%d" % i, staged[:, 0 : PACK * width], width)
             product(1, codes[:], plane[:])
-            for half in range(2):
-                result = tile([P, 2, width], F32, "result%d%d" % (i, half), tag=(("wa00", "wa10"), ("wa01", "wa11"), ("big0", "cap0"))[i][half])
-                for c in range(2):
-                    copy = nc.vector.tensor_copy if last and half == 1 else nc.scalar.copy
-                    copy(result[:, c, :], banks[2 * half + c][:, 0:width])
-                nc.sync.dma_start(out_rows[:, 2 * half : 2 * half + 2, cols], result[:])
+            parts = ((0, 2), (2, 4)) if last else ((0, 4),)
+            for half, (c0, c1) in enumerate(parts):
+                result = tile([P, c1 - c0, width], F32, "result%d%d" % (i, half), tag=spent[i + half])
+                for c in range(c0, c1):
+                    copy = nc.vector.tensor_copy if half == 1 else nc.scalar.copy
+                    copy(result[:, c - c0, :], banks[c][:, 0:width])
+                nc.sync.dma_start(out_rows[:, c0:c1, cols], result[:])

@@ -56,32 +56,32 @@ def tile_list_airway_hazard_features_kernel(
         nc.vector.memset(warm[:, 0:1], 1.0)
         nc.scalar.activation(warm[:, 1:2], warm[:, 0:1], ACT.Ln)
 
-        tab2_w = tile([P, T2], U32, "tab2_w", tag="eight")
-        nc.sync.dma_start(tab2_w[:].bitcast(I32), words_of(tab2_words, 0))
-        wb_raw = tile([P, 2 * H], U8, "wb_raw")
-        nc.sync.dma_start(wb_raw[:].bitcast(I32), wb_words[0].bitcast(I32))
         offs2_t = lists.tile([P, NP // 16], U16, name="offs2_t")
         nc.sync.dma_start(offs2_t[:], offs2)
-        load_planes(nc.sync, tab2_sc, tab2_scales)
-        load_planes(nc.sync, wb_sc_raw, wb_scales)
-        gz_t = tile([P, 2, PACK], F32, "gz_t")
-        ga_t = tile([P, 2, PACK], F32, "ga_t")
-        nc.sync.dma_start(gz_t[:], gz.rearrange("(b p t) -> p b t", b=2, t=PACK))
         pos1_t = lists.tile([P, NP // 16], U16, name="pos1_t")
         nc.sync.dma_start(pos1_t[:], pos1)
         offs_t = lists.tile([P, S // 16], U16, name="offs_t")
         nc.sync.dma_start(offs_t[:], offs)
+        gz_t = tile([P, 2, PACK], F32, "gz_t")
+        ga_t = tile([P, 2, PACK], F32, "ga_t")
+        nc.sync.dma_start(gz_t[:], gz.rearrange("(b p t) -> p b t", b=2, t=PACK))
         nc.sync.dma_start(ga_t[:], ga.rearrange("(b p t) -> p b t", b=2, t=PACK))
+        wb_raw = tile([P, 2 * H], U8, "wb_raw")
+        nc.sync.dma_start(wb_raw[:].bitcast(I32), wb_words[0].bitcast(I32))
+        tab2_w = tile([P, T2], U32, "tab2_w", tag="eight")
+        nc.sync.dma_start(tab2_w[:].bitcast(I32), words_of(tab2_words, 0))
+        load_planes(nc.sync, tab2_sc, tab2_scales)
+        load_planes(nc.sync, wb_sc_raw, wb_scales)
         wgs_t = tile([P, PACK, NP], F32, "wgs_t")
         for q in (0, 2, 1, 3):
             nc.sync.dma_start(wgs_t[32 * q : 32 * q + 32], wgs.rearrange("(u t) j -> u t j", t=PACK))
         load_planes(nc.sync, tab_sc, tab_scales)
 
-        tab_w = []
-        for a in range(2):
-            w = tile([P, T], U32, "tab_w%d" % a, tag="big%d" % a)
-            nc.sync.dma_start(w[:].bitcast(I32), words_of(tab_words, a))
-            tab_w.append(w)
+        tab_w = {}
+
+        def load_tab(a):
+            tab_w[a] = tile([P, T], U32, "tab_w%d" % a, tag="big%d" % a)
+            nc.sync.dma_start(tab_w[a][:].bitcast(I32), words_of(tab_words, a))
 
         wa_raw = {}
         cap_t = {}
@@ -93,11 +93,18 @@ def tile_list_airway_hazard_features_kernel(
                 wa[512 * a : 512 * (a + 1), 512 * b : 512 * (b + 1)].rearrange("(p i) c -> p i c", i=PACK),
             )
 
-        def load_cap(b, tag):
-            cap_t[b] = tile([P, PACK, S], F32, "cap%d" % b, tag=tag)
+        def load_cap(b, h):
             rows = cap[512 * b : 512 * (b + 1), :].rearrange("(p t) j -> p t j", t=PACK)
-            for h in range(2):
-                nc.sync.dma_start(cap_t[b][:, 2 * h : 2 * h + 2, :], rows[:, 2 * h : 2 * h + 2, :])
+            nc.sync.dma_start(cap_t[b][:, 2 * h : 2 * h + 2, :], rows[:, 2 * h : 2 * h + 2, :])
+
+        load_tab(0)
+        load_wa(0, 0)
+        load_wa(1, 0)
+        load_tab(1)
+        cap_t[0] = tile([P, PACK, S], F32, "cap0")
+        for h in range(2):
+            load_wa(h, 1)
+            load_cap(0, h)
 
         wb_codes = tile([P, 2 * H], U8, "wb_codes")
         wb_sc = tile([P, H], U8, "wb_sc")
@@ -114,11 +121,12 @@ def tile_list_airway_hazard_features_kernel(
             wb_sc_raw[:].rearrange("p (b m t) -> p b t m", b=2, t=PACK),
         )
 
-        pages = []
-        for t in range(PACK):
-            page = tile([P, S], F32, "page%d" % t)
-            nc.vector.memset(page[:], 0.0)
-            pages.append(page)
+        pages = {}
+        for key in [(0, t) for t in range(PACK)] + [(1, 0)]:
+            pages[key] = tile([P, S], F32, "page%d%d" % key)
+            nc.vector.memset(pages[key][:], 0.0)
+        for t in range(1, PACK):
+            pages[1, t] = pages[0, t]
 
         gas = {}
         for b in range(2):
@@ -139,9 +147,9 @@ def tile_list_airway_hazard_features_kernel(
                 nc.scalar.activation(gas[b, t][:], gas[b, t][:], ACT.Ln, bias=1.0)
 
         def scatter(b, t, weight):
-            nc.vector.tensor_tensor(pages[t][:].indirect(pos1_t[:]), gas[b, t][:], weight, ALU.mult)
+            nc.vector.tensor_tensor(pages[b, t][:].indirect(pos1_t[:]), gas[b, t][:], weight, ALU.mult)
 
-        for t in range(PACK - 1):
+        for t in range(PACK):
             weight = tile([P, NP], F32, "weight%d" % t)
             nc.vector.tensor_scalar(weight[:], wgs_t[:, t, :], gz_t[:, 0, t : t + 1], None, ALU.mult)
             scatter(0, t, weight[:])
@@ -150,17 +158,6 @@ def tile_list_airway_hazard_features_kernel(
         v_sc = tile([P, S], U8, "v_sc")
         nc.vector.tensor_copy(v_sc[:], tab_sc[:].indirect(offs_t[:]))
         nc.vector.tensor_copy(v[0][:], tab_w[0][:].indirect(offs_t[:]))
-        nc.vector.tensor_copy(v[1][:], tab_w[1][:].indirect(offs_t[:]))
-
-        load_wa(0, 0)
-        load_wa(1, 0)
-        load_cap(0, "cap0")
-        load_wa(0, 1)
-        load_wa(1, 1)
-        wc_raw = tile([P, 2, PACK, N], F32, "wc_raw", tag="big0")
-        for b in range(2):
-            nc.sync.dma_start(wc_raw[:, b], wc[512 * b : 512 * (b + 1), :].rearrange("(p t) n -> p t n", t=PACK))
-        load_cap(1, "big1")
 
         def quantize(name, staged, width):
             codes = tile([P, width], U32, name + "_codes")
@@ -178,17 +175,24 @@ def tile_list_airway_hazard_features_kernel(
             wa_q[a, b] = quantize("wa%d%d" % (a, b), staged, BANK)
 
         def staging():
-            return tile([P, PACK * BANK], BF16, "staged", bufs=2)
+            return tile([P, PACK * BANK], BF16, "staged", bufs=3)
 
         quantize_wa(0, 0, staging()[:])
-        held = tile([P, 2 * BANK], F32, "held")
-        quantize_wa(1, 0, held[:].bitcast(BF16))
-        t = PACK - 1
-        nc.vector.tensor_scalar(held[:, 0:NP], wgs_t[:, t, :], gz_t[:, 0, t : t + 1], None, ALU.mult)
-        scatter(0, t, held[:, 0:NP])
+        quantize_wa(1, 0, staging()[:])
+        nc.vector.tensor_copy(v[1][:], tab_w[1][:].indirect(offs_t[:]))
+        held = tile([P, NP], F32, "held", tag="big1")
+        nc.vector.tensor_scalar(held[:], wgs_t[:, 0, :], gz_t[:, 1, 0:1], None, ALU.mult)
+        scatter(1, 0, held[:])
+
+        wc_raw = tile([P, 2, PACK, N], F32, "wc_raw", tag="big0")
+        for b in range(2):
+            nc.sync.dma_start(wc_raw[:, b], wc[512 * b : 512 * (b + 1), :].rearrange("(p t) n -> p t n", t=PACK))
+        cap_t[1] = tile([P, PACK, S], F32, "cap1", tag="big1")
+        for h in range(2):
+            load_cap(1, h)
 
         def sensor_features(b, t):
-            act = tile([P, S], F32, "act", bufs=5)
+            act = tile([P, S], F32, "act", bufs=6)
             for h in range(2):
                 cols = slice(BANK * h, BANK * (h + 1))
                 acc = psum.tile([P, BANK], F32, name="acc", tag="acc")
@@ -207,17 +211,13 @@ def tile_list_airway_hazard_features_kernel(
             return act
 
         def cap_and_add(b, acts, z_rows, cols):
-            def capped(t):
+            for t in range(PACK):
                 nc.vector.scalar_tensor_tensor(
                     acts[t][:, cols], acts[t][:, cols], ga_t[:, b, t : t + 1], cap_t[b][:, t, cols], ALU.mult, ALU.min
                 )
-
-            capped(0)
             for t in range(PACK):
-                if t + 1 < PACK:
-                    capped(t + 1)
                 nc.vector.scalar_tensor_tensor(
-                    z_rows[:, t, cols], acts[t][:, cols], gz_t[:, b, t : t + 1], pages[t][:, cols], ALU.mult, ALU.add
+                    z_rows[:, t, cols], acts[t][:, cols], gz_t[:, b, t : t + 1], pages[b, t][:, cols], ALU.mult, ALU.add
                 )
 
         def interleave(copy, staged, rows):
@@ -232,7 +232,7 @@ def tile_list_airway_hazard_features_kernel(
         z_rows = tile([P, PACK, S], BF16, "z_rows0", tag="eight")
         cap_and_add(0, acts, z_rows, slice(0, S))
 
-        for t in range(PACK):
+        for t in range(1, PACK):
             nc.scalar.activation(wgs_t[:, t, :], wgs_t[:, t, :], ACT.Copy, scale=gz_t[:, 1, t : t + 1])
         acts = [sensor_features(1, t) for t in range(PACK)]
         z0_codes = tile([P, S], U32, "z0_codes")
@@ -247,7 +247,7 @@ def tile_list_airway_hazard_features_kernel(
             staged = tile([P, PACK * N], BF16, "wc_staged%d" % b, tag="wa%d0" % b)
             interleave(nc.scalar.copy, staged[:], wc_raw[:, b])
             wc_q.append(quantize("wc%d" % b, staged[:], N))
-        for t in range(PACK):
+        for t in range(1, PACK):
             scatter(1, t, wgs_t[:, t, :])
 
         z_rows = tile([P, PACK, S], BF16, "z_rows1", tag="eight")

@@ -1,6 +1,7 @@
 from contextlib import ExitStack
 
 import concourse.mybir as mybir
+from concourse.masks import make_identity
 
 K, K2, T, T2, S, NP, H, N = 1024, 512, 4096, 2048, 1024, 512, 1024, 512
 FLOPS = 2 * (K * H * S + K2 * H * NP + H * N * S)
@@ -19,6 +20,7 @@ ACT = mybir.ActivationFunctionType
 P = 128
 PACK = 4
 BANK = 512
+TURNED = 1024
 LAST_CHUNKS = ((0, 256), (256, 256), (512, 256), (768, 128), (896, 128))
 
 
@@ -52,6 +54,8 @@ def tile_list_airway_hazard_features_kernel(
         nc.gpsimd.memset(tab2_sc[:].bitcast(I32), 0)
         nc.gpsimd.memset(wb_sc_raw[:].bitcast(I32), 0)
         nc.gpsimd.memset(tab_sc[:].bitcast(I32), 0)
+        identity = tile([P, P], F32, "identity")
+        make_identity(nc, identity[:])
         warm = tile([P, 8], F32, "warm")
         nc.vector.memset(warm[:, 0:1], 1.0)
         nc.scalar.activation(warm[:, 1:2], warm[:, 0:1], ACT.Ln)
@@ -126,10 +130,11 @@ def tile_list_airway_hazard_features_kernel(
             pages[key] = tile([P, S], F32, "page%d%d" % key)
             nc.vector.memset(pages[key][:], 0.0)
         for t in range(1, PACK):
-            pages[1, t] = pages[0, t]
+            pages[1, t] = pages[0, t - 1]
 
         gas = {}
-        for b in range(2):
+
+        def gas_features(b):
             for t in range(PACK):
                 s = PACK * b + t
                 acc = psum.tile([P, NP], F32, name="acc", tag="acc")
@@ -146,15 +151,17 @@ def tile_list_airway_hazard_features_kernel(
                 nc.scalar.activation(gas[b, t][:], acc[:], ACT.Square)
                 nc.scalar.activation(gas[b, t][:], gas[b, t][:], ACT.Ln, bias=1.0)
 
+        gas_features(0)
+
         def scatter(b, t, weight):
             nc.vector.tensor_tensor(pages[b, t][:].indirect(pos1_t[:]), gas[b, t][:], weight, ALU.mult)
 
-        for t in range(PACK):
+        for t in range(PACK - 1):
             weight = tile([P, NP], F32, "weight%d" % t)
             nc.vector.tensor_scalar(weight[:], wgs_t[:, t, :], gz_t[:, 0, t : t + 1], None, ALU.mult)
             scatter(0, t, weight[:])
 
-        v = [tile([P, S], U32, "v%d" % a) for a in range(2)]
+        v = [tile([P, S], U32, "v0")]
         v_sc = tile([P, S], U8, "v_sc")
         nc.vector.tensor_copy(v_sc[:], tab_sc[:].indirect(offs_t[:]))
         nc.vector.tensor_copy(v[0][:], tab_w[0][:].indirect(offs_t[:]))
@@ -178,11 +185,17 @@ def tile_list_airway_hazard_features_kernel(
             return tile([P, PACK * BANK], BF16, "staged", bufs=3)
 
         quantize_wa(0, 0, staging()[:])
-        quantize_wa(1, 0, staging()[:])
+        quantize_wa(1, 0, tile([P, PACK * BANK], BF16, "staged10", tag="v1")[:])
+        gas_features(1)
+        v.append(tile([P, S], U32, "v1"))
         nc.vector.tensor_copy(v[1][:], tab_w[1][:].indirect(offs_t[:]))
-        held = tile([P, NP], F32, "held", tag="big1")
-        nc.vector.tensor_scalar(held[:], wgs_t[:, 0, :], gz_t[:, 1, 0:1], None, ALU.mult)
-        scatter(1, 0, held[:])
+        held = tile([P, 2, NP], F32, "held", tag="big1")
+        nc.vector.tensor_scalar(held[:, 0, :], wgs_t[:, 3, :], gz_t[:, 0, 3:4], None, ALU.mult)
+        nc.scalar.activation(held[:, 1, :], wgs_t[:, 0, :], ACT.Copy, scale=gz_t[:, 1, 0:1])
+        scatter(0, 3, held[:, 0, :])
+        scatter(1, 0, held[:, 1, :])
+
+        nc.scalar.activation(wgs_t[:, 1, :], wgs_t[:, 1, :], ACT.Copy, scale=gz_t[:, 1, 1:2])
 
         wc_raw = tile([P, 2, PACK, N], F32, "wc_raw", tag="big0")
         for b in range(2):
@@ -192,7 +205,7 @@ def tile_list_airway_hazard_features_kernel(
             load_cap(1, h)
 
         def sensor_features(b, t):
-            act = tile([P, S], F32, "act", bufs=6)
+            act = tile([P, S], F32, "act", bufs=7)
             for h in range(2):
                 cols = slice(BANK * h, BANK * (h + 1))
                 acc = psum.tile([P, BANK], F32, name="acc", tag="acc")
@@ -210,11 +223,13 @@ def tile_list_airway_hazard_features_kernel(
                 nc.scalar.activation(act[:, cols], acc[:], ACT.Silu)
             return act
 
-        def cap_and_add(b, acts, z_rows, cols):
+        def cap_features(b, acts, cols):
             for t in range(PACK):
                 nc.vector.scalar_tensor_tensor(
                     acts[t][:, cols], acts[t][:, cols], ga_t[:, b, t : t + 1], cap_t[b][:, t, cols], ALU.mult, ALU.min
                 )
+
+        def add_pages(b, acts, z_rows, cols):
             for t in range(PACK):
                 nc.vector.scalar_tensor_tensor(
                     z_rows[:, t, cols], acts[t][:, cols], gz_t[:, b, t : t + 1], pages[b, t][:, cols], ALU.mult, ALU.add
@@ -228,29 +243,60 @@ def tile_list_airway_hazard_features_kernel(
 
         acts = [sensor_features(0, t) for t in range(PACK)]
         quantize_wa(0, 1, staging()[:])
-        quantize_wa(1, 1, staging()[:])
-        z_rows = tile([P, PACK, S], BF16, "z_rows0", tag="eight")
-        cap_and_add(0, acts, z_rows, slice(0, S))
+        late = tile([P, 2, NP], F32, "late", tag="staged", bufs=3)
+        quantize_wa(1, 1, late[:].rearrange("p t j -> p (t j)").bitcast(BF16))
+        nc.vector.tensor_scalar(late[:, 0, :], wgs_t[:, 2, :], gz_t[:, 1, 2:3], None, ALU.mult)
+        nc.scalar.activation(late[:, 1, :], wgs_t[:, 3, :], ACT.Copy, scale=gz_t[:, 1, 3:4])
+        cap_features(0, acts, slice(0, S))
 
-        for t in range(1, PACK):
-            nc.scalar.activation(wgs_t[:, t, :], wgs_t[:, t, :], ACT.Copy, scale=gz_t[:, 1, t : t + 1])
+        groups = TURNED // (2 * P)
+        turned = tile([P, TURNED // P, 2, P, 2], BF16, "turned", tag="eight")
+        for u in range(2):
+            banks = [psum.tile([P, 2, 2, P], F32, name="res", tag="res") for g in range(groups)]
+            for e in range(2):
+                t = 2 * u + e
+                nc.scalar.activation(acts[t][:, 0:TURNED], acts[t][:, 0:TURNED], ACT.Copy, scale=gz_t[:, 0, t : t + 1])
+                for c in range(TURNED // P):
+                    cols = slice(P * c, P * (c + 1))
+                    for term, first in ((acts[t], True), (pages[0, t], False)):
+                        nc.tensor.matmul(
+                            banks[c // 2][:, c % 2, e, :], term[:, cols], identity[:],
+                            start=first, stop=not first, is_transpose=True,
+                        )
+            for g in range(groups):
+                nc.scalar.copy(turned[:, 2 * g : 2 * g + 2, u], banks[g][:].rearrange("j c e p -> j c p e"))
+
         acts = [sensor_features(1, t) for t in range(PACK)]
         z0_codes = tile([P, S], U32, "z0_codes")
         z0_sc = tile([P, S], U8, "z0_sc")
-        for h in range(2):
+        for h in (0, 1):
             cols = slice(BANK * h, BANK * (h + 1))
             staged = staging()
-            interleave(nc.scalar.copy, staged[:], z_rows[:, :, cols])
+            if BANK * h >= TURNED:
+                interleave(nc.scalar.copy, staged[:], z_rows[:, :, cols])
+            else:
+                pairs = turned[:].rearrange("j c u p e -> j (c u p e)").bitcast(F32)
+                for g in range(2):
+                    bank = psum.tile([P, 2, 2, P], F32, name="res", tag="res")
+                    for c in range(2):
+                        for u in range(2):
+                            w0 = P * (2 * (4 * h + 2 * g + c) + u)
+                            nc.tensor.transpose(bank[:, c, u, :], pairs[:, w0 : w0 + P], identity[:])
+                    nc.scalar.copy(
+                        staged[:].bitcast(F32)[:, BANK * g : BANK * (g + 1)].rearrange("p (c j u) -> p c j u", c=2, u=2),
+                        bank[:].rearrange("p c u j -> p c j u"),
+                    )
             nc.vector.quantize_mx(out=z0_codes[:, cols].bitcast(FP8X4), scales=z0_sc[:, cols], in_=staged[:])
         wc_q = []
         for b in range(2):
             staged = tile([P, PACK * N], BF16, "wc_staged%d" % b, tag="wa%d0" % b)
             interleave(nc.scalar.copy, staged[:], wc_raw[:, b])
             wc_q.append(quantize("wc%d" % b, staged[:], N))
-        for t in range(1, PACK):
-            scatter(1, t, wgs_t[:, t, :])
+        scatter(1, 1, wgs_t[:, 1, :])
+        for t in (2, 3):
+            scatter(1, t, late[:, t - 2, :])
 
-        z_rows = tile([P, PACK, S], BF16, "z_rows1", tag="eight")
+        z_rows = tile([P, PACK, S], BF16, "z_rows1", tag="cap0")
         spent = ("wa01", "wa11", "wa00", "wa10", "big0", "cap0")
         out_rows = out.rearrange("(c p) j -> p c j", p=P)
         for i, (j0, width) in enumerate(LAST_CHUNKS):
@@ -272,7 +318,8 @@ def tile_list_airway_hazard_features_kernel(
                     )
 
             product(0, z0_codes[:, cols], z0_sc[:, cols])
-            cap_and_add(1, acts, z_rows, cols)
+            cap_features(1, acts, cols)
+            add_pages(1, acts, z_rows, cols)
             staged = staging()
             interleave(nc.vector.tensor_copy if narrow else nc.scalar.copy, staged[:, 0 : PACK * width], z_rows[:, :, cols])
             codes, plane = quantize("z1%d" % i, staged[:, 0 : PACK * width], width)

@@ -51,14 +51,15 @@ def tile_list_airway_hazard_features_kernel(
         tab2_sc = tile([P, T2], U8, "tab2_sc")
         wb_sc_raw = tile([P, H], U8, "wb_sc_raw")
         tab_sc = tile([P, T], U8, "tab_sc")
+        one = tile([P, 1], F32, "one")
+        zero = tile([P, 1], F32, "zero")
+        nc.vector.memset(one[:], 1.0)
+        nc.scalar.activation(zero[:], one[:], ACT.Ln)
         nc.gpsimd.memset(tab2_sc[:].bitcast(I32), 0)
         nc.gpsimd.memset(wb_sc_raw[:].bitcast(I32), 0)
-        nc.gpsimd.memset(tab_sc[:].bitcast(I32), 0)
+        nc.vector.memset(tab_sc[:].bitcast(I32), 0)
         identity = tile([P, P], F32, "identity")
         make_identity(nc, identity[:])
-        warm = tile([P, 8], F32, "warm")
-        nc.vector.memset(warm[:, 0:1], 1.0)
-        nc.scalar.activation(warm[:, 1:2], warm[:, 0:1], ACT.Ln)
 
         offs2_t = lists.tile([P, NP // 16], U16, name="offs2_t")
         nc.sync.dma_start(offs2_t[:], offs2)
@@ -148,8 +149,8 @@ def tile_list_airway_hazard_features_kernel(
                     stop=True,
                 )
                 gas[b, t] = tile([P, NP], F32, "gas%d%d" % (b, t))
-                nc.scalar.activation(gas[b, t][:], acc[:], ACT.Square)
-                nc.scalar.activation(gas[b, t][:], gas[b, t][:], ACT.Ln, bias=1.0)
+                nc.scalar.activation(gas[b, t][:], acc[:], ACT.Square, bias=zero[:])
+                nc.scalar.activation(gas[b, t][:], gas[b, t][:], ACT.Ln, bias=one[:])
 
         gas_features(0)
 
@@ -297,7 +298,7 @@ def tile_list_airway_hazard_features_kernel(
             scatter(1, t, late[:, t - 2, :])
 
         z_rows = tile([P, PACK, S], BF16, "z_rows1", tag="cap0")
-        spent = ("wa01", "wa11", "wa00", "wa10", "big0", "cap0")
+        spent = ("wa01", "wa11", "wa00", "wa10", "big0", "big1")
         out_rows = out.rearrange("(c p) j -> p c j", p=P)
         for i, (j0, width) in enumerate(LAST_CHUNKS):
             cols = slice(j0, j0 + width)

from contextlib import ExitStack

import concourse.mybir as mybir
from concourse.masks import make_identity

K, K2, T, T2, S, NP, H, N = 1024, 512, 4096, 2048, 1024, 512, 1024, 512
FLOPS = 2 * (K * H * S + K2 * H * NP + H * N * S)

F32 = mybir.dt.float32
BF16 = mybir.dt.bfloat16
I32 = mybir.dt.int32
U32 = mybir.dt.uint32
U16 = mybir.dt.uint16
U8 = mybir.dt.uint8
FP8X4 = mybir.dt.float8_e4m3fn_x4
FP4X4 = mybir.dt.float4_e2m1fn_x4
ALU = mybir.AluOpType
ACT = mybir.ActivationFunctionType

P = 128
PACK = 4
BANK = 512
TURNED = 1024
LAST_CHUNKS = ((0, 256), (256, 256), (512, 256), (768, 128), (896, 128))


def tile_list_airway_hazard_features_kernel(
    tc, tab_words, tab_scales, offs, tab2_words, tab2_scales, offs2, pos1,
    wa, ga, wb_words, wb_scales, wgs, cap, gz, wc, out,
):
    nc = tc.nc
    with ExitStack() as ctx:
        lists = ctx.enter_context(tc.tile_pool(name="lists", bufs=1))
        keep = ctx.enter_context(tc.tile_pool(name="keep", bufs=1))
        psum = ctx.enter_context(tc.psum_pool(name="psum", bufs=4))

        def tile(shape, dtype, name, tag=None, bufs=1):
            return keep.tile(shape, dtype, name=name, tag=tag or name, bufs=bufs, align_bytes=64)

        def load_planes(queue, plane, scales):
            rows = PACK * scales.shape[0]
            for q in range(4):
                queue.dma_start(
                    plane[32 * q : 32 * q + rows, :].bitcast(I32),
                    scales[:, 4 * q : 4 * q + 4, :].bitcast(I32),
                )

        def words_of(words, a):
            return words[a].rearrange("p n t -> p (n t)").bitcast(I32)

        tab2_sc = tile([P, T2], U8, "tab2_sc")
        wb_sc_raw = tile([P, H], U8, "wb_sc_raw")
        tab_sc = tile([P, T], U8, "tab_sc")
        one = tile([P, 1], F32, "one")
        zero = tile([P, 1], F32, "zero")
        nc.vector.memset(one[:], 1.0)
        nc.scalar.activation(zero[:], one[:], ACT.Ln)
        nc.gpsimd.memset(tab2_sc[:].bitcast(I32), 0)
        nc.gpsimd.memset(wb_sc_raw[:].bitcast(I32), 0)
        nc.vector.memset(tab_sc[:].bitcast(I32), 0)
        identity = tile([P, P], F32, "identity")
        make_identity(nc, identity[:])

        offs2_t = lists.tile([P, NP // 16], U16, name="offs2_t")
        nc.sync.dma_start(offs2_t[:], offs2)
        pos1_t = lists.tile([P, NP // 16], U16, name="pos1_t")
        nc.sync.dma_start(pos1_t[:], pos1)
        offs_t = lists.tile([P, S // 16], U16, name="offs_t")
        nc.sync.dma_start(offs_t[:], offs)
        gz_t = tile([P, 2, PACK], F32, "gz_t")
        ga_t = tile([P, 2, PACK], F32, "ga_t")
        nc.sync.dma_start(gz_t[:], gz.rearrange("(b p t) -> p b t", b=2, t=PACK))
        nc.sync.dma_start(ga_t[:], ga.rearrange("(b p t) -> p b t", b=2, t=PACK))
        wb_raw = tile([P, 2 * H], U8, "wb_raw")
        nc.sync.dma_start(wb_raw[:].bitcast(I32), wb_words[0].bitcast(I32))
        tab2_w = tile([P, T2], U32, "tab2_w", tag="eight")
        nc.sync.dma_start(tab2_w[:].bitcast(I32), words_of(tab2_words, 0))
        load_planes(nc.sync, tab2_sc, tab2_scales)
        load_planes(nc.sync, wb_sc_raw, wb_scales)
        wgs_t = tile([P, PACK, NP], F32, "wgs_t")
        for q in (0, 2, 1, 3):
            nc.sync.dma_start(wgs_t[32 * q : 32 * q + 32], wgs.rearrange("(u t) j -> u t j", t=PACK))
        load_planes(nc.sync, tab_sc, tab_scales)

        tab_w = {}

        def load_tab(a):
            tab_w[a] = tile([P, T], U32, "tab_w%d" % a, tag="big%d" % a)
            nc.sync.dma_start(tab_w[a][:].bitcast(I32), words_of(tab_words, a))

        wa_raw = {}
        cap_t = {}

        def load_wa(a, b):
            wa_raw[a, b] = tile([P, PACK, BANK], F32, "wa_raw%d%d" % (a, b), tag="wa%d%d" % (a, b))
            nc.sync.dma_start(
                wa_raw[a, b][:],
                wa[512 * a : 512 * (a + 1), 512 * b : 512 * (b + 1)].rearrange("(p i) c -> p i c", i=PACK),
            )

        def load_cap(b, h):
            rows = cap[512 * b : 512 * (b + 1), :].rearrange("(p t) j -> p t j", t=PACK)
            nc.sync.dma_start(cap_t[b][:, 2 * h : 2 * h + 2, :], rows[:, 2 * h : 2 * h + 2, :])

        load_tab(0)
        load_wa(0, 0)
        load_wa(1, 0)
        load_tab(1)
        cap_t[0] = tile([P, PACK, S], F32, "cap0")
        for h in range(2):
            load_wa(h, 1)
            load_cap(0, h)

        wb_codes = tile([P, 2 * H], U8, "wb_codes")
        wb_sc = tile([P, H], U8, "wb_sc")
        nc.vector.tensor_copy(
            wb_codes[:].bitcast(U16).rearrange("p (b t m) -> p b t m", b=2, t=PACK),
            wb_raw[:].bitcast(U16).rearrange("p (b m t) -> p b t m", b=2, t=PACK),
        )
        v2 = tile([P, NP], U32, "v2")
        v2_sc = tile([P, NP], U8, "v2_sc")
        nc.vector.tensor_copy(v2[:], tab2_w[:].indirect(offs2_t[:]))
        nc.vector.tensor_copy(v2_sc[:], tab2_sc[:].indirect(offs2_t[:]))
        nc.vector.tensor_copy(
            wb_sc[:].rearrange("p (b t m) -> p b t m", b=2, t=PACK),
            wb_sc_raw[:].rearrange("p (b m t) -> p b t m", b=2, t=PACK),
        )

        pages = {}
        for key in [(0, t) for t in range(PACK)] + [(1, 0)]:
            pages[key] = tile([P, S], F32, "page%d%d" % key)
            nc.vector.memset(pages[key][:], 0.0)
        for t in range(1, PACK):
            pages[1, t] = pages[0, t - 1]

        gas = {}

        def gas_features(b):
            for t in range(PACK):
                s = PACK * b + t
                acc = psum.tile([P, NP], F32, name="acc", tag="acc")
                nc.tensor.matmul_mx(
                    out=acc[:],
                    lhsT=wb_codes[:, 2 * P * s : 2 * P * (s + 1)].bitcast(FP4X4),
                    lhsT_scale=wb_sc[:, P * s : P * (s + 1)],
                    rhs=v2[:].bitcast(FP8X4),
                    rhs_scale=v2_sc[:],
                    start=True,
                    stop=True,
                )
                gas[b, t] = tile([P, NP], F32, "gas%d%d" % (b, t))
                nc.scalar.activation(gas[b, t][:], acc[:], ACT.Square, bias=zero[:])
                nc.scalar.activation(gas[b, t][:], gas[b, t][:], ACT.Ln, bias=one[:])

        gas_features(0)

        def scatter(b, t, weight):
            nc.vector.tensor_tensor(pages[b, t][:].indirect(pos1_t[:]), gas[b, t][:], weight, ALU.mult)

        for t in range(PACK - 1):
            weight = tile([P, NP], F32, "weight%d" % t)
            nc.vector.tensor_scalar(weight[:], wgs_t[:, t, :], gz_t[:, 0, t : t + 1], None, ALU.mult)
            scatter(0, t, weight[:])

        v = [tile([P, S], U32, "v0")]
        v_sc = tile([P, S], U8, "v_sc")
        nc.vector.tensor_copy(v_sc[:], tab_sc[:].indirect(offs_t[:]))
        nc.vector.tensor_copy(v[0][:], tab_w[0][:].indirect(offs_t[:]))

        def quantize(name, staged, width):
            codes = tile([P, width], U32, name + "_codes")
            plane = tile([P, width], U8, name + "_sc")
            nc.vector.quantize_mx(out=codes[:].bitcast(FP8X4), scales=plane[:], in_=staged)
            return codes, plane

        wa_q = {}

        def quantize_wa(a, b, staged):
            nc.scalar.copy(
                staged.rearrange("p (t m i) -> p m i t", t=PACK, i=PACK),
                wa_raw[a, b][:].rearrange("p i (m t) -> p m i t", t=PACK),
            )
            wa_q[a, b] = quantize("wa%d%d" % (a, b), staged, BANK)

        def staging():
            return tile([P, PACK * BANK], BF16, "staged", bufs=3)

        quantize_wa(0, 0, staging()[:])
        quantize_wa(1, 0, tile([P, PACK * BANK], BF16, "staged10", tag="v1")[:])
        gas_features(1)
        v.append(tile([P, S], U32, "v1"))
        nc.vector.tensor_copy(v[1][:], tab_w[1][:].indirect(offs_t[:]))
        held = tile([P, 2, NP], F32, "held", tag="big1")
        nc.vector.tensor_scalar(held[:, 0, :], wgs_t[:, 3, :], gz_t[:, 0, 3:4], None, ALU.mult)
        nc.scalar.activation(held[:, 1, :], wgs_t[:, 0, :], ACT.Copy, scale=gz_t[:, 1, 0:1])
        scatter(0, 3, held[:, 0, :])
        scatter(1, 0, held[:, 1, :])

        nc.scalar.activation(wgs_t[:, 1, :], wgs_t[:, 1, :], ACT.Copy, scale=gz_t[:, 1, 1:2])

        wc_raw = tile([P, 2, PACK, N], F32, "wc_raw", tag="big0")
        for b in range(2):
            nc.sync.dma_start(wc_raw[:, b], wc[512 * b : 512 * (b + 1), :].rearrange("(p t) n -> p t n", t=PACK))
        cap_t[1] = tile([P, PACK, S], F32, "cap1", tag="big1")
        for h in range(2):
            load_cap(1, h)

        def sensor_features(b, t):
            act = tile([P, S], F32, "act", bufs=7)
            for h in range(2):
                cols = slice(BANK * h, BANK * (h + 1))
                acc = psum.tile([P, BANK], F32, name="acc", tag="acc")
                for a in range(2):
                    codes, plane = wa_q[a, b]
                    nc.tensor.matmul_mx(
                        out=acc[:],
                        lhsT=codes[:, P * t : P * (t + 1)].bitcast(FP8X4),
                        lhsT_scale=plane[:, P * t : P * (t + 1)],
                        rhs=v[a][:, cols].bitcast(FP8X4),
                        rhs_scale=v_sc[4 * a : P, cols],
                        start=(a == 0),
                        stop=(a == 1),
                    )
                nc.scalar.activation(act[:, cols], acc[:], ACT.Silu)
            return act

        def cap_features(b, acts, cols):
            for t in range(PACK):
                nc.vector.scalar_tensor_tensor(
                    acts[t][:, cols], acts[t][:, cols], ga_t[:, b, t : t + 1], cap_t[b][:, t, cols], ALU.mult, ALU.min
                )

        def add_pages(b, acts, z_rows, cols):
            for t in range(PACK):
                nc.vector.scalar_tensor_tensor(
                    z_rows[:, t, cols], acts[t][:, cols], gz_t[:, b, t : t + 1], pages[b, t][:, cols], ALU.mult, ALU.add
                )

        def interleave(copy, staged, rows):
            copy(
                staged.rearrange("p (c e t) -> p c t e", e=4, t=PACK),
                rows.rearrange("p t (c e) -> p c t e", e=4),
            )

        acts = [sensor_features(0, t) for t in range(PACK)]
        quantize_wa(0, 1, staging()[:])
        late = tile([P, 2, NP], F32, "late", tag="staged", bufs=3)
        quantize_wa(1, 1, late[:].rearrange("p t j -> p (t j)").bitcast(BF16))
        nc.vector.tensor_scalar(late[:, 0, :], wgs_t[:, 2, :], gz_t[:, 1, 2:3], None, ALU.mult)
        nc.scalar.activation(late[:, 1, :], wgs_t[:, 3, :], ACT.Copy, scale=gz_t[:, 1, 3:4])
        cap_features(0, acts, slice(0, S))

        groups = TURNED // (2 * P)
        turned = tile([P, TURNED // P, 2, P, 2], BF16, "turned", tag="eight")
        for u in range(2):
            banks = [psum.tile([P, 2, 2, P], F32, name="res", tag="res") for g in range(groups)]
            for e in range(2):
                t = 2 * u + e
                nc.scalar.activation(acts[t][:, 0:TURNED], acts[t][:, 0:TURNED], ACT.Copy, scale=gz_t[:, 0, t : t + 1])
                for c in range(TURNED // P):
                    cols = slice(P * c, P * (c + 1))
                    for term, first in ((acts[t], True), (pages[0, t], False)):
                        nc.tensor.matmul(
                            banks[c // 2][:, c % 2, e, :], term[:, cols], identity[:],
                            start=first, stop=not first, is_transpose=True,
                        )
            for g in range(groups):
                nc.scalar.copy(turned[:, 2 * g : 2 * g + 2, u], banks[g][:].rearrange("j c e p -> j c p e"))

        acts = [sensor_features(1, t) for t in range(PACK)]
        z0_codes = tile([P, S], U32, "z0_codes")
        z0_sc = tile([P, S], U8, "z0_sc")
        for h in (0, 1):
            cols = slice(BANK * h, BANK * (h + 1))
            staged = staging()
            if BANK * h >= TURNED:
                interleave(nc.scalar.copy, staged[:], z_rows[:, :, cols])
            else:
                pairs = turned[:].rearrange("j c u p e -> j (c u p e)").bitcast(F32)
                for g in range(2):
                    bank = psum.tile([P, 2, 2, P], F32, name="res", tag="res")
                    for c in range(2):
                        for u in range(2):
                            w0 = P * (2 * (4 * h + 2 * g + c) + u)
                            nc.tensor.transpose(bank[:, c, u, :], pairs[:, w0 : w0 + P], identity[:])
                    nc.scalar.copy(
                        staged[:].bitcast(F32)[:, BANK * g : BANK * (g + 1)].rearrange("p (c j u) -> p c j u", c=2, u=2),
                        bank[:].rearrange("p c u j -> p c j u"),
                    )
            nc.vector.quantize_mx(out=z0_codes[:, cols].bitcast(FP8X4), scales=z0_sc[:, cols], in_=staged[:])
        wc_q = []
        for b in range(2):
            staged = tile([P, PACK * N], BF16, "wc_staged%d" % b, tag="wa%d0" % b)
            interleave(nc.scalar.copy, staged[:], wc_raw[:, b])
            wc_q.append(quantize("wc%d" % b, staged[:], N))
        scatter(1, 1, wgs_t[:, 1, :])
        for t in (2, 3):
            scatter(1, t, late[:, t - 2, :])

        z_rows = tile([P, PACK, S], BF16, "z_rows1", tag="cap0")
        spent = ("wa01", "wa11", "wa00", "wa10", "big0", "big1")
        out_rows = out.rearrange("(c p) j -> p c j", p=P)
        for i, (j0, width) in enumerate(LAST_CHUNKS):
            cols = slice(j0, j0 + width)
            last = i == len(LAST_CHUNKS) - 1
            narrow = width < 256
            banks = [psum.tile([P, BANK], F32, name="res", tag=("res", "acc")[i % 2]) for c in range(4)]

            def product(b, codes, plane):
                for c in range(4):
                    nc.tensor.matmul_mx(
                        out=banks[c][:, 0:width],
                        lhsT=wc_q[b][0][:, P * c : P * (c + 1)].bitcast(FP8X4),
                        lhsT_scale=wc_q[b][1][:, P * c : P * (c + 1)],
                        rhs=codes.bitcast(FP8X4),
                        rhs_scale=plane,
                        start=(b == 0),
                        stop=(b == 1),
                    )

            product(0, z0_codes[:, cols], z0_sc[:, cols])
            cap_features(1, acts, cols)
            add_pages(1, acts, z_rows, cols)
            staged = staging()
            interleave(nc.vector.tensor_copy if narrow else nc.scalar.copy, staged[:, 0 : PACK * width], z_rows[:, :, cols])
            codes, plane = quantize("z1%d" % i, staged[:, 0 : PACK * width], width)
            product(1, codes[:], plane[:])
            parts = ((0, 2), (2, 4)) if last else ((0, 4),)
            for half, (c0, c1) in enumerate(parts):
                result = tile([P, c1 - c0, width], F32, "result%d%d" % (i, half), tag=spent[i + half])
                for c in range(c0, c1):
                    copy = nc.vector.tensor_copy if half == 1 else nc.scalar.copy
                    copy(result[:, c - c0, :], banks[c][:, 0:width])
                nc.sync.dma_start(out_rows[:, c0:c1, cols], result[:])
